import numpy as np
import ml_dtypes


def mxq(x, axis, fmt="e4m3"):
    dtype, down = {"e4m3": (ml_dtypes.float8_e4m3fn, 7), "e5m2": (ml_dtypes.float8_e5m2, 14)}[fmt]
    v = np.moveaxis(np.asarray(x, np.float32).astype(ml_dtypes.bfloat16).astype(np.float64), axis, -1)
    blocks = v.reshape(v.shape[:-1] + (-1, 32))
    amax = np.abs(blocks).max(-1, keepdims=True)
    byte = np.maximum(np.where(amax > 0, np.frexp(amax)[1] - 1 + 127, 0) - down, 1)
    scale = np.exp2(byte - 127.0)
    codes = (blocks / scale).astype(np.float32).astype(dtype).astype(np.float64)
    return np.moveaxis((codes * scale).reshape(v.shape), -1, axis)


WIDE = False


def mx_kscale(k):
    if not WIDE:
        return np.ones(k)
    levels = np.array([10, -10, 5, -5, 0])
    if k % 512:
        return np.exp2(np.random.permutation(np.resize(levels, k // 32))).repeat(32)
    a = np.empty((k // 512, 16))
    for p in range(k // 512):
        a[p, :8] = np.random.permutation(np.resize(levels, 8))
        for g in range(8):
            far = levels[np.abs(levels - a[p, g]) >= 10]
            a[p, g + 8] = far[np.random.randint(len(far))]
    return np.exp2(a.ravel()).repeat(32)


def f64(x):
    return np.asarray(x).astype(np.float64)


def striped(idx):
    return np.tile(idx.reshape(-1, 16).T, (8, 1)).astype(np.uint16)


def unstriped(offs):
    return offs[:16].T.reshape(-1).astype(np.int64)


def striped8(idx):
    return np.concatenate([x.reshape(-1, 16).T for x in idx]).astype(np.uint16)


def runs(offs, k):
    lists = np.stack([offs[16 * r : 16 * r + 16].T.reshape(-1) for r in range(8)]).astype(np.int64)
    return lists[np.arange(k) % 512 // 64]


def pack_weight(w):
    k, n = w.shape
    w = f64(np.asarray(w, np.float32).astype(ml_dtypes.bfloat16)).reshape(k // 32, 32, n)
    amax = np.abs(w).max(1)
    byte = np.clip(np.where(amax > 0, np.frexp(amax)[1] - 1 + 127 - 7, 1), 1, 254)
    scaled = (w * np.exp2(127.0 - byte)[:, None, :]).reshape(k, n).astype(np.float32)
    words = np.ascontiguousarray(scaled.reshape(k // 512, 128, 4, n).transpose(0, 1, 3, 2)).astype(ml_dtypes.float8_e4m3fn).view(np.uint8)
    return words, np.ascontiguousarray(byte.astype(np.uint8).reshape(k // 512, 16, n))


def unpack_weight(words, scales):
    g, p, n, _ = words.shape
    vals = np.ascontiguousarray(words).view(ml_dtypes.float8_e4m3fn).astype(np.float64) * np.repeat(np.exp2(scales.astype(np.float64) - 127.0), 8, axis=1)[..., None]
    return vals.transpose(0, 1, 3, 2).reshape(g * 512, n)


def sigmoid(v):
    return 1.0 / (1.0 + np.exp(-np.maximum(v, -700.0)))


K, T, S, N, H = 512, 2048, 512, 512, 512


def setup_inputs():
    n = np.random.standard_normal
    s = mx_kscale(K)[:, None]
    u = mx_kscale(H)
    packed_xT = pack_weight(n((K, T)) * s)
    return {
        "x_words": packed_xT[0],
        "x_scales": packed_xT[1],
        "w1": (n((K, H)) / np.sqrt(K) / s).astype(np.float32),
        "w2": (n((K, H)) / np.sqrt(K) / s).astype(np.float32),
        "gn": (np.random.uniform(0.5, 1.5, (H, 1)) * u[:, None]).astype(np.float32),
        "w3": (n((H, N)) / np.sqrt(H) / u[:, None]).astype(np.float32),
        "offs": striped(np.random.permutation(T)[:S]),
        "two": striped(np.random.permutation(T)[:S]),
        "b1": striped8(np.stack([np.random.permutation(S) for _ in range(8)])),
        "b3": striped8(np.stack([np.random.permutation(S) for _ in range(8)])),
        "b4": striped8(np.stack([np.random.permutation(S) for _ in range(8)])),
    }


def reference(x_words, x_scales, w1, w2, gn, w3, offs, two, b1, b3, b4):
    x_two = unpack_weight(x_words, x_scales)[:, unstriped(two)]
    c = sigmoid(mxq(f64(w2), 0, "e4m3").T @ x_two)
    v1 = c[np.arange(H)[:, None], runs(b1, H)]
    xq = unpack_weight(x_words, x_scales)[:, unstriped(offs)]
    y = mxq(f64(w1), 0, "e4m3").T @ xq
    v3 = c[np.arange(H)[:, None], runs(b3, H)]
    v4 = c[np.arange(H)[:, None], runs(b4, H)]
    z = f64(gn) * ((v1 * (y[np.arange(H)[:, None], runs(b1, H)]) + v3 * (y[np.arange(H)[:, None], runs(b3, H)]) + v4 * (y[np.arange(H)[:, None], runs(b4, H)])) / (v1 + v3 + v4))
    return mxq(f64(w3), 0, "e4m3").T @ mxq(z, 0, "e4m3")

@@ -1,0 +1,213 @@
+from contextlib import ExitStack
+
+import concourse.mybir as mybir
+from concourse.masks import make_identity
+
+F32 = mybir.dt.float32
+BF16 = mybir.dt.bfloat16
+I32 = mybir.dt.int32
+U32 = mybir.dt.uint32
+U16 = mybir.dt.uint16
+U8 = mybir.dt.uint8
+FP8X4 = mybir.dt.float8_e4m3fn_x4
+ACT = mybir.ActivationFunctionType
+ALU = mybir.AluOpType
+
+P = 128
+T = 2048
+S = 512
+PACK = 4
+RUNS = 8
+GROUP = 16
+TILES = 4
+CHUNKS = S // P
+VECTOR_DEN_LISTS = [3,0,0,0]
+
+FLOPS = 3 * 2 * 512 * 512 * 512
+
+
+def tile_picked_vwap3_none_p_kernel(tc, x_words, x_scales, w1, w2, gn, w3, offs, two, b1, b3, b4, out):
+    nc = tc.nc
+    with ExitStack() as ctx:
+        keep = ctx.enter_context(tc.tile_pool(name="keep", bufs=1))
+        psum = ctx.enter_context(tc.psum_pool(name="psum", bufs=1))
+
+        def sb(name, shape, dtype):
+            return keep.tile(shape, dtype, name=name, align_bytes=64)
+
+        def bank(n, name, shape):
+            return psum.tile(shape, F32, name=name, tag="bank%d" % n)
+
+        x_plane = sb("x_plane", [P, T], U8)
+        nc.vector.memset(x_plane[:].bitcast(I32), 0)
+        warm = sb("warm", [P, 1], F32)
+        nc.vector.memset(warm[:], 0.0)
+        for q in range(4):
+            nc.scalar.dma_start(out=x_plane[32 * q : 32 * q + 4, :].bitcast(I32), in_=x_scales[0, 4 * q : 4 * q + 4, :].bitcast(I32))
+        warm_out = sb("warm_out", [P, 1], F32)
+        nc.scalar.activation(warm_out[:], warm[:], ACT.Sigmoid)
+
+        def load_list(name, src):
+            tile = keep.tile([P, S // GROUP], U16, name=name)
+            nc.sync.dma_start(tile[:], src)
+            return tile
+
+        def load_halves(name, w):
+            halves = []
+            for h in range(2):
+                raw = sb("%s_raw%d" % (name, h), [P, PACK, 256], F32)
+                nc.sync.dma_start(out=raw[:], in_=w.rearrange("(p j) c -> p j c", j=PACK)[:, :, 256 * h : 256 * (h + 1)])
+                halves.append(raw)
+            return halves
+
+        two_l = load_list("two_l", two)
+        x_tab = sb("x_tab", [P, T], U32)
+        nc.sync.dma_start(out=x_tab[:].bitcast(I32), in_=x_words[0].rearrange("p c r -> p (c r)").bitcast(I32))
+        w2_raw = load_halves("w2", w2)
+        offs_l = load_list("offs_l", offs)
+        w1_raw = load_halves("w1", w1)
+        lists = [load_list("b1_l", b1), load_list("b3_l", b3), load_list("b4_l", b4)]
+        gain = [sb("gain%d" % t, [P, 1], F32) for t in range(TILES)]
+        with nc.allow_non_contiguous_dma(reason="one gain to a partition"):
+            for t in range(TILES):
+                nc.sync.dma_start(out=gain[t][:], in_=gn.rearrange("(r t q) o -> t r q o", r=RUNS, t=TILES)[t])
+        w3_raw = sb("w3_raw", [P, PACK, 512], F32)
+        nc.sync.dma_start(out=w3_raw[:], in_=w3.rearrange("(p j) c -> p j c", j=PACK))
+
+        ident = sb("ident", [P, P], F32)
+        make_identity(nc, ident[:])
+
+        a_win = [sb("a_win%d" % t, [P, 2 * S], F32) if VECTOR_DEN_LISTS[t] < 3 else None for t in range(TILES)]
+        c_win = [sb("c_win%d" % t, [P, 2 * S], F32) if VECTOR_DEN_LISTS[t] > 0 else None for t in range(TILES)]
+        p_win = [sb("p_win%d" % t, [P, 2 * S], F32) for t in range(TILES)]
+        c_of = []
+        for t in range(TILES):
+            if c_win[t] is None:
+                c_of.append(a_win[t][:, S:])
+            else:
+                c_of.append(c_win[t][:, :S])
+                nc.gpsimd.memset(c_win[t][:, S:], 0.0)
+                if a_win[t] is not None:
+                    nc.gpsimd.memset(a_win[t][:, S:], 0.0)
+            nc.gpsimd.memset(p_win[t][:, S:], 0.0)
+
+        def pick(name, table, dtype, lst):
+            picked = sb(name, [P, S], dtype)
+            nc.vector.tensor_copy(picked[:], table[:].indirect(lst[:]))
+            return picked
+
+        def cast(engine, dst, src):
+            if engine is nc.scalar:
+                nc.scalar.copy(dst, src)
+            else:
+                engine.tensor_copy(dst, src)
+
+        def cast_half(grouped, halves, h, engines):
+            for t in range(TILES):
+                dst = grouped[t][:, 256 * h : 256 * (h + 1)].rearrange("p (r a i j) -> p r a j i", r=4, a=4, i=4)
+                src = halves[h][:].rearrange("p j (r t a i) -> p t r a j i", r=4, t=TILES, a=4)[:, t]
+                cast(engines[t], dst, src)
+
+        def quantize_tile(name, grouped):
+            codes = sb(name + "_c", [P, P], U32)
+            scales = sb(name + "_s", [P, P], U8)
+            nc.vector.quantize_mx(out=codes[:].bitcast(FP8X4), scales=scales[:], in_=grouped[:])
+            return codes, scales
+
+        def product(acc, lhs_codes, lhs_scales, rhs_codes, rhs_scales):
+            nc.tensor.matmul_mx(out=acc, lhsT=lhs_codes.bitcast(FP8X4), lhsT_scale=lhs_scales,
+                                rhs=rhs_codes.bitcast(FP8X4), rhs_scale=rhs_scales, start=True, stop=True)
+
+        x2_scales = pick("x2_scales", x_plane, U8, two_l)
+        x2_words = pick("x2_words", x_tab, U32, two_l)
+        x1_scales = pick("x1_scales", x_plane, U8, offs_l)
+        w2_g = [sb("w2_g%d" % t, [P, P * PACK], BF16) for t in range(TILES)]
+        w1_g = [sb("w1_g%d" % t, [P, P * PACK], BF16) for t in range(TILES)]
+        cast_half(w2_g, w2_raw, 0, [nc.scalar] * TILES)
+        cast_half(w2_g, w2_raw, 1, [nc.vector, nc.vector, nc.scalar, nc.scalar])
+        w2_q = [quantize_tile("w2_%d" % t, w2_g[t]) for t in range(TILES)]
+        cast_half(w1_g, w1_raw, 0, [nc.scalar] * TILES)
+        x1_words = pick("x1_words", x_tab, U32, offs_l)
+        a_bank = [bank(t, "a_bank%d" % t, [P, S]) for t in range(TILES)]
+        for t in range(TILES):
+            product(a_bank[t][:], w2_q[t][0][:], w2_q[t][1][:], x2_words[:], x2_scales[:])
+            nc.scalar.activation(c_of[t], a_bank[t][:], ACT.Sigmoid)
+            if a_win[t] is not None:
+                nc.scalar.copy(a_win[t][:, :S], a_bank[t][:])
+
+        cast_half(w1_g, w1_raw, 1, [nc.vector] * TILES)
+        w1_q = [quantize_tile("w1_%d" % t, w1_g[t]) for t in range(TILES)]
+        y_bank = [bank(4 + t, "y_bank%d" % t, [P, S]) for t in range(TILES)]
+        for t in range(TILES):
+            product(y_bank[t][:], w1_q[t][0][:], w1_q[t][1][:], x1_words[:], x1_scales[:])
+
+        def chunk(tile, jc):
+            return tile[:, jc * P : (jc + 1) * P]
+
+        den_log = sb("den_log", [P, CHUNKS, RUNS, TILES, GROUP], F32)
+        num_bank = [None] * CHUNKS
+        den_bank = [None] * TILES
+
+        def den_tile(t):
+            vols = []
+            for n in range(3):
+                vol = sb("vol%d_%d" % (t, n), [P, S], F32)
+                if n < VECTOR_DEN_LISTS[t]:
+                    nc.vector.tensor_copy(vol[:], c_win[t][:].indirect(lists[n][:]))
+                else:
+                    nc.scalar.activation(vol[:], a_win[t][:].indirect(lists[n][:]), ACT.Sigmoid)
+                vols.append(vol)
+            den_bank[t] = bank(4 + t, "den_bank%d" % t, [P, CHUNKS, P])
+            for jc in range(CHUNKS):
+                for n in range(3):
+                    nc.tensor.matmul(den_bank[t][:, jc, :], lhsT=chunk(vols[n], jc), rhs=ident[:], is_transpose=True, start=(n == 0), stop=(n == 2))
+
+        def num_tile(t):
+            for n in range(3):
+                paid = sb("paid%d_%d" % (t, n), [P, S], F32)
+                nc.vector.tensor_copy(paid[:], p_win[t][:].indirect(lists[n][:]))
+                for jc in range(CHUNKS):
+                    nc.tensor.matmul(num_bank[jc][:, :, t, :], lhsT=chunk(paid, jc), rhs=ident[:], is_transpose=True, start=(n == 0), stop=(n == 2))
+
+        for t in range(TILES):
+            nc.vector.scalar_tensor_tensor(out=p_win[t][:, :S], in0=y_bank[t][:], scalar=gain[t][:], in1=c_of[t], op0=ALU.mult, op1=ALU.mult)
+        for jc in range(CHUNKS):
+            num_bank[jc] = bank(jc, "num_bank%d" % jc, [P, RUNS, TILES, GROUP])
+
+        w3_g = sb("w3_g", [P, 512 * PACK], BF16)
+        w3_codes = sb("w3_codes", [P, 512], U32)
+        w3_scales = sb("w3_scales", [P, 512], U8)
+        for t in range(TILES):
+            den_tile(t)
+            num_tile(t)
+            if t == 1:
+                nc.vector.tensor_copy(w3_g[:].rearrange("p (a i j) -> p a j i", i=4, j=PACK), w3_raw[:].rearrange("p j (a i) -> p a j i", i=4))
+            if t == 2:
+                nc.vector.quantize_mx(out=w3_codes[:].bitcast(FP8X4), scales=w3_scales[:], in_=w3_g[:])
+
+        for t in range(TILES):
+            nc.scalar.activation(den_log[:, :, :, t, :], den_bank[t][:].rearrange("p c (r q) -> p c r q", q=GROUP), ACT.Ln)
+
+        out_view = out.rearrange("(m p) j -> p m j", p=P)
+        z_rows, z_group, z_codes, z_scales = [], [], [], []
+        for jc in range(CHUNKS):
+            inv = sb("inv%d" % jc, [P, S], F32)
+            nc.scalar.activation(inv[:], den_log[:, jc].rearrange("p r t q -> p (r t q)"), ACT.Exp, scale=-1.0)
+            z_rows.append(sb("z_rows%d" % jc, [P, S], BF16))
+            nc.vector.tensor_tensor(out=z_rows[jc][:], in0=num_bank[jc][:].rearrange("p r t q -> p (r t q)"), in1=inv[:], op=ALU.mult)
+        for jc in range(CHUNKS):
+            back = bank(4 + jc % 2, "back%d" % jc, [P, 2, P])
+            words = z_rows[jc][:].bitcast(F32)
+            for u in range(2):
+                nc.tensor.transpose(back[:, u, :], words[:, u : 256 : 2], ident[:])
+            z_group.append(sb("z_group%d" % jc, [P, P * PACK], BF16))
+            nc.vector.tensor_copy(z_group[jc][:].bitcast(F32).rearrange("p (j u) -> p j u", u=2), back[:].rearrange("p u j -> p j u"))
+            z_codes.append(sb("z_codes%d" % jc, [P, P], U32))
+            z_scales.append(sb("z_scales%d" % jc, [P, P], U8))
+            nc.vector.quantize_mx(out=z_codes[jc][:].bitcast(FP8X4), scales=z_scales[jc][:], in_=z_group[jc][:])
+            acc = bank(6 + jc % 2, "acc%d" % jc, [P, TILES, P])
+            for m in range(TILES):
+                product(acc[:, m, :], chunk(w3_codes, m), chunk(w3_scales, m), z_codes[jc][:], z_scales[jc][:])
+            res = sb("res%d" % jc, [P, TILES, P], F32)
+            nc.scalar.copy(res[:], acc[:])
+            nc.sync.dma_start(out=out_view[:, :, jc * P : (jc + 1) * P], in_=res[:])

@@ -21,7 +21,7 @@ RUNS = 8
 GROUP = 16
 TILES = 4
 CHUNKS = S // P
-VECTOR_DEN_LISTS = [3,0,0,0]
+VECTOR_DEN_LISTS = [2,0,0,0]
 
 FLOPS = 3 * 2 * 512 * 512 * 512
 
@@ -39,11 +39,9 @@ def tile_picked_vwap3_none_p_kernel(tc, x_words, x_scales, w1, w2, gn, w3, offs,
             return psum.tile(shape, F32, name=name, tag="bank%d" % n)
 
         x_plane = sb("x_plane", [P, T], U8)
-        nc.vector.memset(x_plane[:].bitcast(I32), 0)
+        nc.gpsimd.memset(x_plane[:].bitcast(I32), 0)
         warm = sb("warm", [P, 1], F32)
         nc.vector.memset(warm[:], 0.0)
-        for q in range(4):
-            nc.scalar.dma_start(out=x_plane[32 * q : 32 * q + 4, :].bitcast(I32), in_=x_scales[0, 4 * q : 4 * q + 4, :].bitcast(I32))
         warm_out = sb("warm_out", [P, 1], F32)
         nc.scalar.activation(warm_out[:], warm[:], ACT.Sigmoid)
 
@@ -52,20 +50,20 @@ def tile_picked_vwap3_none_p_kernel(tc, x_words, x_scales, w1, w2, gn, w3, offs,
             nc.sync.dma_start(tile[:], src)
             return tile
 
-        def load_halves(name, w):
-            halves = []
-            for h in range(2):
-                raw = sb("%s_raw%d" % (name, h), [P, PACK, 256], F32)
-                nc.sync.dma_start(out=raw[:], in_=w.rearrange("(p j) c -> p j c", j=PACK)[:, :, 256 * h : 256 * (h + 1)])
-                halves.append(raw)
-            return halves
+        def load_half(name, w, h):
+            raw = sb("%s_raw%d" % (name, h), [P, PACK, 256], F32)
+            nc.sync.dma_start(out=raw[:], in_=w.rearrange("(p j) c -> p j c", j=PACK)[:, :, 256 * h : 256 * (h + 1)])
+            return raw
 
         two_l = load_list("two_l", two)
         x_tab = sb("x_tab", [P, T], U32)
         nc.sync.dma_start(out=x_tab[:].bitcast(I32), in_=x_words[0].rearrange("p c r -> p (c r)").bitcast(I32))
-        w2_raw = load_halves("w2", w2)
+        for q in range(4):
+            nc.sync.dma_start(out=x_plane[32 * q : 32 * q + 4, :].bitcast(I32), in_=x_scales[0, 4 * q : 4 * q + 4, :].bitcast(I32))
+        w2_raw = [load_half("w2", w2, h) for h in range(2)]
+        w1_raw = [load_half("w1", w1, 0)]
         offs_l = load_list("offs_l", offs)
-        w1_raw = load_halves("w1", w1)
+        w1_raw.append(load_half("w1", w1, 1))
         lists = [load_list("b1_l", b1), load_list("b3_l", b3), load_list("b4_l", b4)]
         gain = [sb("gain%d" % t, [P, 1], F32) for t in range(TILES)]
         with nc.allow_non_contiguous_dma(reason="one gain to a partition"):
@@ -104,9 +102,14 @@ def tile_picked_vwap3_none_p_kernel(tc, x_words, x_scales, w1, w2, gn, w3, offs,
 
         def cast_half(grouped, halves, h, engines):
             for t in range(TILES):
-                dst = grouped[t][:, 256 * h : 256 * (h + 1)].rearrange("p (r a i j) -> p r a j i", r=4, a=4, i=4)
-                src = halves[h][:].rearrange("p j (r t a i) -> p t r a j i", r=4, t=TILES, a=4)[:, t]
-                cast(engines[t], dst, src)
+                if engines[t] is nc.gpsimd:
+                    dst = grouped[t][:, 256 * h : 256 * (h + 1)].rearrange("p (r q j) -> p r q j", r=4, j=PACK)
+                    src = halves[h][:].rearrange("p j (r t q) -> p t r q j", r=4, t=TILES)[:, t]
+                    nc.gpsimd.tensor_scalar(dst, src, 1.0, 0.0, op0=ALU.mult, op1=ALU.add)
+                else:
+                    dst = grouped[t][:, 256 * h : 256 * (h + 1)].rearrange("p (r a i j) -> p r a j i", r=4, a=4, i=4)
+                    src = halves[h][:].rearrange("p j (r t a i) -> p t r a j i", r=4, t=TILES, a=4)[:, t]
+                    cast(engines[t], dst, src)
 
         def quantize_tile(name, grouped):
             codes = sb(name + "_c", [P, P], U32)
@@ -118,15 +121,15 @@ def tile_picked_vwap3_none_p_kernel(tc, x_words, x_scales, w1, w2, gn, w3, offs,
             nc.tensor.matmul_mx(out=acc, lhsT=lhs_codes.bitcast(FP8X4), lhsT_scale=lhs_scales,
                                 rhs=rhs_codes.bitcast(FP8X4), rhs_scale=rhs_scales, start=True, stop=True)
 
-        x2_scales = pick("x2_scales", x_plane, U8, two_l)
         x2_words = pick("x2_words", x_tab, U32, two_l)
-        x1_scales = pick("x1_scales", x_plane, U8, offs_l)
+        x2_scales = pick("x2_scales", x_plane, U8, two_l)
         w2_g = [sb("w2_g%d" % t, [P, P * PACK], BF16) for t in range(TILES)]
         w1_g = [sb("w1_g%d" % t, [P, P * PACK], BF16) for t in range(TILES)]
         cast_half(w2_g, w2_raw, 0, [nc.scalar] * TILES)
         cast_half(w2_g, w2_raw, 1, [nc.vector, nc.vector, nc.scalar, nc.scalar])
         w2_q = [quantize_tile("w2_%d" % t, w2_g[t]) for t in range(TILES)]
-        cast_half(w1_g, w1_raw, 0, [nc.scalar] * TILES)
+        cast_half(w1_g, w1_raw, 0, [nc.gpsimd] * TILES)
+        x1_scales = pick("x1_scales", x_plane, U8, offs_l)
         x1_words = pick("x1_words", x_tab, U32, offs_l)
         a_bank = [bank(t, "a_bank%d" % t, [P, S]) for t in range(TILES)]
         for t in range(TILES):
@@ -151,7 +154,7 @@ def tile_picked_vwap3_none_p_kernel(tc, x_words, x_scales, w1, w2, gn, w3, offs,
         def den_tile(t):
             vols = []
             for n in range(3):
-                vol = sb("vol%d_%d" % (t, n), [P, S], F32)
+                vol = keep.tile([P, S], F32, name="vol%d_%d" % (t, n), tag="vol%d_%d" % (t, n), align_bytes=64)
                 if n < VECTOR_DEN_LISTS[t]:
                     nc.vector.tensor_copy(vol[:], c_win[t][:].indirect(lists[n][:]))
                 else:
@@ -162,12 +165,12 @@ def tile_picked_vwap3_none_p_kernel(tc, x_words, x_scales, w1, w2, gn, w3, offs,
                 for n in range(3):
                     nc.tensor.matmul(den_bank[t][:, jc, :], lhsT=chunk(vols[n], jc), rhs=ident[:], is_transpose=True, start=(n == 0), stop=(n == 2))
 
-        def num_tile(t):
+        def num_tile(t, identity):
             for n in range(3):
                 paid = sb("paid%d_%d" % (t, n), [P, S], F32)
                 nc.vector.tensor_copy(paid[:], p_win[t][:].indirect(lists[n][:]))
                 for jc in range(CHUNKS):
-                    nc.tensor.matmul(num_bank[jc][:, :, t, :], lhsT=chunk(paid, jc), rhs=ident[:], is_transpose=True, start=(n == 0), stop=(n == 2))
+                    nc.tensor.matmul(num_bank[jc][:, :, t, :], lhsT=chunk(paid, jc), rhs=identity[:], is_transpose=True, start=(n == 0), stop=(n == 2))
 
         for t in range(TILES):
             nc.vector.scalar_tensor_tensor(out=p_win[t][:, :S], in0=y_bank[t][:], scalar=gain[t][:], in1=c_of[t], op0=ALU.mult, op1=ALU.mult)
@@ -179,9 +182,12 @@ def tile_picked_vwap3_none_p_kernel(tc, x_words, x_scales, w1, w2, gn, w3, offs,
         w3_scales = sb("w3_scales", [P, 512], U8)
         for t in range(TILES):
             den_tile(t)
-            num_tile(t)
-            if t == 1:
-                nc.vector.tensor_copy(w3_g[:].rearrange("p (a i j) -> p a j i", i=4, j=PACK), w3_raw[:].rearrange("p j (a i) -> p a j i", i=4))
+        late_ident = keep.tile([P, P], F32, name="late_ident", tag="vol3_2", align_bytes=64)
+        nc.gpsimd.tensor_copy(late_ident[:], ident[:])
+        for t in range(TILES):
+            num_tile(t, ident if t < 2 else late_ident)
+            if t == 0:
+                nc.gpsimd.tensor_scalar(w3_g[:].rearrange("p (c j) -> p c j", j=PACK), w3_raw[:].rearrange("p j c -> p c j"), 1.0, 0.0, op0=ALU.mult, op1=ALU.add)
             if t == 2:
                 nc.vector.quantize_mx(out=w3_codes[:].bitcast(FP8X4), scales=w3_scales[:], in_=w3_g[:])
 
@@ -201,13 +207,15 @@ def tile_picked_vwap3_none_p_kernel(tc, x_words, x_scales, w1, w2, gn, w3, offs,
             for u in range(2):
                 nc.tensor.transpose(back[:, u, :], words[:, u : 256 : 2], ident[:])
             z_group.append(sb("z_group%d" % jc, [P, P * PACK], BF16))
-            nc.vector.tensor_copy(z_group[jc][:].bitcast(F32).rearrange("p (j u) -> p j u", u=2), back[:].rearrange("p u j -> p j u"))
+            nc.scalar.copy(z_group[jc][:].bitcast(F32).rearrange("p (j u) -> p j u", u=2), back[:].rearrange("p u j -> p j u"))
+        for jc in range(CHUNKS):
             z_codes.append(sb("z_codes%d" % jc, [P, P], U32))
             z_scales.append(sb("z_scales%d" % jc, [P, P], U8))
             nc.vector.quantize_mx(out=z_codes[jc][:].bitcast(FP8X4), scales=z_scales[jc][:], in_=z_group[jc][:])
+        for jc in range(CHUNKS):
             acc = bank(6 + jc % 2, "acc%d" % jc, [P, TILES, P])
             for m in range(TILES):
                 product(acc[:, m, :], chunk(w3_codes, m), chunk(w3_scales, m), z_codes[jc][:], z_scales[jc][:])
             res = sb("res%d" % jc, [P, TILES, P], F32)
-            nc.scalar.copy(res[:], acc[:])
+            cast(nc.scalar if jc % 2 == 0 else nc.vector, res[:], acc[:])
             nc.sync.dma_start(out=out_view[:, :, jc * P : (jc + 1) * P], in_=res[:])

@@ -70,7 +70,8 @@ def tile_picked_vwap3_none_p_kernel(tc, x_words, x_scales, w1, w2, gn, w3, offs,
             for t in range(TILES):
                 nc.sync.dma_start(out=gain[t][:], in_=gn.rearrange("(r t q) o -> t r q o", r=RUNS, t=TILES)[t])
         w3_raw = sb("w3_raw", [P, PACK, 512], F32)
-        nc.sync.dma_start(out=w3_raw[:], in_=w3.rearrange("(p j) c -> p j c", j=PACK))
+        for u in range(2):
+            nc.sync.dma_start(out=w3_raw[:, 2 * u : 2 * u + 2, :].rearrange("p e c -> p (e c)"), in_=w3.rearrange("(b u q e) c -> u b q (e c)", u=2, q=8, e=2)[u])
 
         ident = sb("ident", [P, P], F32)
         make_identity(nc, ident[:])
@@ -124,7 +125,8 @@ def tile_picked_vwap3_none_p_kernel(tc, x_words, x_scales, w1, w2, gn, w3, offs,
         x2_words = pick("x2_words", x_tab, U32, two_l)
         x2_scales = pick("x2_scales", x_plane, U8, two_l)
         w2_g = [sb("w2_g%d" % t, [P, P * PACK], BF16) for t in range(TILES)]
-        w1_g = [sb("w1_g%d" % t, [P, P * PACK], BF16) for t in range(TILES)]
+        w1_all = sb("w1_all", [P, TILES * P * PACK], BF16)
+        w1_g = [w1_all[:, t * 512 : (t + 1) * 512] for t in range(TILES)]
         cast_half(w2_g, w2_raw, 0, [nc.scalar] * TILES)
         cast_half(w2_g, w2_raw, 1, [nc.vector, nc.vector, nc.scalar, nc.scalar])
         w2_q = [quantize_tile("w2_%d" % t, w2_g[t]) for t in range(TILES)]
@@ -139,15 +141,17 @@ def tile_picked_vwap3_none_p_kernel(tc, x_words, x_scales, w1, w2, gn, w3, offs,
                 nc.scalar.copy(a_win[t][:, :S], a_bank[t][:])
 
         cast_half(w1_g, w1_raw, 1, [nc.vector] * TILES)
-        w1_q = [quantize_tile("w1_%d" % t, w1_g[t]) for t in range(TILES)]
+        w1_codes = sb("w1_codes", [P, 512], U32)
+        w1_scales = sb("w1_scales", [P, 512], U8)
+        nc.vector.quantize_mx(out=w1_codes[:].bitcast(FP8X4), scales=w1_scales[:], in_=w1_all[:])
         y_bank = [bank(4 + t, "y_bank%d" % t, [P, S]) for t in range(TILES)]
         for t in range(TILES):
-            product(y_bank[t][:], w1_q[t][0][:], w1_q[t][1][:], x1_words[:], x1_scales[:])
+            product(y_bank[t][:], w1_codes[:, t * P : (t + 1) * P], w1_scales[:, t * P : (t + 1) * P], x1_words[:], x1_scales[:])
 
         def chunk(tile, jc):
             return tile[:, jc * P : (jc + 1) * P]
 
-        den_log = sb("den_log", [P, CHUNKS, RUNS, TILES, GROUP], F32)
+        den_log = sb("den_log", [P, CHUNKS, 2, RUNS, 2, GROUP], F32)
         num_bank = [None] * CHUNKS
         den_bank = [None] * TILES
 
@@ -170,12 +174,12 @@ def tile_picked_vwap3_none_p_kernel(tc, x_words, x_scales, w1, w2, gn, w3, offs,
                 paid = sb("paid%d_%d" % (t, n), [P, S], F32)
                 nc.vector.tensor_copy(paid[:], p_win[t][:].indirect(lists[n][:]))
                 for jc in range(CHUNKS):
-                    nc.tensor.matmul(num_bank[jc][:, :, t, :], lhsT=chunk(paid, jc), rhs=identity[:], is_transpose=True, start=(n == 0), stop=(n == 2))
+                    nc.tensor.matmul(num_bank[jc][:, t % 2, :, t // 2, :], lhsT=chunk(paid, jc), rhs=identity[:], is_transpose=True, start=(n == 0), stop=(n == 2))
 
         for t in range(TILES):
             nc.vector.scalar_tensor_tensor(out=p_win[t][:, :S], in0=y_bank[t][:], scalar=gain[t][:], in1=c_of[t], op0=ALU.mult, op1=ALU.mult)
         for jc in range(CHUNKS):
-            num_bank[jc] = bank(jc, "num_bank%d" % jc, [P, RUNS, TILES, GROUP])
+            num_bank[jc] = bank(jc, "num_bank%d" % jc, [P, 2, RUNS, 2, GROUP])
 
         w3_g = sb("w3_g", [P, 512 * PACK], BF16)
         w3_codes = sb("w3_codes", [P, 512], U32)
@@ -183,7 +187,10 @@ def tile_picked_vwap3_none_p_kernel(tc, x_words, x_scales, w1, w2, gn, w3, offs,
         for t in range(TILES):
             den_tile(t)
         late_ident = keep.tile([P, P], F32, name="late_ident", tag="vol3_2", align_bytes=64)
-        nc.gpsimd.tensor_copy(late_ident[:], ident[:])
+        for t in range(TILES):
+            nc.scalar.activation(den_log[:, :, t % 2, :, t // 2, :], den_bank[t][:].rearrange("p c (r q) -> p c r q", q=GROUP), ACT.Ln)
+            if t == 0:
+                nc.scalar.copy(late_ident[:], ident[:])
         for t in range(TILES):
             num_tile(t, ident if t < 2 else late_ident)
             if t == 0:
@@ -191,21 +198,19 @@ def tile_picked_vwap3_none_p_kernel(tc, x_words, x_scales, w1, w2, gn, w3, offs,
             if t == 2:
                 nc.vector.quantize_mx(out=w3_codes[:].bitcast(FP8X4), scales=w3_scales[:], in_=w3_g[:])
 
-        for t in range(TILES):
-            nc.scalar.activation(den_log[:, :, :, t, :], den_bank[t][:].rearrange("p c (r q) -> p c r q", q=GROUP), ACT.Ln)
 
         out_view = out.rearrange("(m p) j -> p m j", p=P)
         z_rows, z_group, z_codes, z_scales = [], [], [], []
         for jc in range(CHUNKS):
             inv = sb("inv%d" % jc, [P, S], F32)
-            nc.scalar.activation(inv[:], den_log[:, jc].rearrange("p r t q -> p (r t q)"), ACT.Exp, scale=-1.0)
+            nc.scalar.activation(inv[:], den_log[:, jc].rearrange("p u r h q -> p (u r h q)"), ACT.Exp, scale=-1.0)
             z_rows.append(sb("z_rows%d" % jc, [P, S], BF16))
-            nc.vector.tensor_tensor(out=z_rows[jc][:], in0=num_bank[jc][:].rearrange("p r t q -> p (r t q)"), in1=inv[:], op=ALU.mult)
+            nc.vector.tensor_tensor(out=z_rows[jc][:], in0=num_bank[jc][:].rearrange("p u r h q -> p (u r h q)"), in1=inv[:], op=ALU.mult)
         for jc in range(CHUNKS):
             back = bank(4 + jc % 2, "back%d" % jc, [P, 2, P])
             words = z_rows[jc][:].bitcast(F32)
             for u in range(2):
-                nc.tensor.transpose(back[:, u, :], words[:, u : 256 : 2], ident[:])
+                nc.tensor.transpose(back[:, u, :], chunk(words, u), ident[:])
             z_group.append(sb("z_group%d" % jc, [P, P * PACK], BF16))
             nc.scalar.copy(z_group[jc][:].bitcast(F32).rearrange("p (j u) -> p j u", u=2), back[:].rearrange("p u j -> p j u"))
         for jc in range(CHUNKS):
@@ -217,5 +222,5 @@ def tile_picked_vwap3_none_p_kernel(tc, x_words, x_scales, w1, w2, gn, w3, offs,
             for m in range(TILES):
                 product(acc[:, m, :], chunk(w3_codes, m), chunk(w3_scales, m), z_codes[jc][:], z_scales[jc][:])
             res = sb("res%d" % jc, [P, TILES, P], F32)
-            cast(nc.scalar if jc % 2 == 0 else nc.vector, res[:], acc[:])
+            cast(nc.scalar if jc < CHUNKS - 1 else nc.vector, res[:], acc[:])
             nc.sync.dma_start(out=out_view[:, :, jc * P : (jc + 1) * P], in_=res[:])

from contextlib import ExitStack

import concourse.mybir as mybir
from concourse.masks import make_identity

F32 = mybir.dt.float32
BF16 = mybir.dt.bfloat16
I32 = mybir.dt.int32
U32 = mybir.dt.uint32
U16 = mybir.dt.uint16
U8 = mybir.dt.uint8
FP8X4 = mybir.dt.float8_e4m3fn_x4
ACT = mybir.ActivationFunctionType
ALU = mybir.AluOpType

P = 128
T = 2048
S = 512
PACK = 4
RUNS = 8
GROUP = 16
TILES = 4
CHUNKS = S // P
VECTOR_DEN_LISTS = [2,0,0,0]

FLOPS = 3 * 2 * 512 * 512 * 512


def tile_picked_vwap3_none_p_kernel(tc, x_words, x_scales, w1, w2, gn, w3, offs, two, b1, b3, b4, out):
    nc = tc.nc
    with ExitStack() as ctx:
        keep = ctx.enter_context(tc.tile_pool(name="keep", bufs=1))
        psum = ctx.enter_context(tc.psum_pool(name="psum", bufs=1))

        def sb(name, shape, dtype):
            return keep.tile(shape, dtype, name=name, align_bytes=64)

        def bank(n, name, shape):
            return psum.tile(shape, F32, name=name, tag="bank%d" % n)

        x_plane = sb("x_plane", [P, T], U8)
        nc.gpsimd.memset(x_plane[:].bitcast(I32), 0)
        warm = sb("warm", [P, 1], F32)
        nc.vector.memset(warm[:], 0.0)
        warm_out = sb("warm_out", [P, 1], F32)
        nc.scalar.activation(warm_out[:], warm[:], ACT.Sigmoid)

        def load_list(name, src):
            tile = keep.tile([P, S // GROUP], U16, name=name)
            nc.sync.dma_start(tile[:], src)
            return tile

        def load_half(name, w, h):
            raw = sb("%s_raw%d" % (name, h), [P, PACK, 256], F32)
            nc.sync.dma_start(out=raw[:], in_=w.rearrange("(p j) c -> p j c", j=PACK)[:, :, 256 * h : 256 * (h + 1)])
            return raw

        two_l = load_list("two_l", two)
        x_tab = sb("x_tab", [P, T], U32)
        nc.sync.dma_start(out=x_tab[:].bitcast(I32), in_=x_words[0].rearrange("p c r -> p (c r)").bitcast(I32))
        for q in range(4):
            nc.sync.dma_start(out=x_plane[32 * q : 32 * q + 4, :].bitcast(I32), in_=x_scales[0, 4 * q : 4 * q + 4, :].bitcast(I32))
        w2_raw = [load_half("w2", w2, h) for h in range(2)]
        w1_raw = [load_half("w1", w1, 0)]
        offs_l = load_list("offs_l", offs)
        w1_raw.append(load_half("w1", w1, 1))
        lists = [load_list("b1_l", b1), load_list("b3_l", b3), load_list("b4_l", b4)]
        gain = [sb("gain%d" % t, [P, 1], F32) for t in range(TILES)]
        with nc.allow_non_contiguous_dma(reason="one gain to a partition"):
            for t in range(TILES):
                nc.sync.dma_start(out=gain[t][:], in_=gn.rearrange("(r t q) o -> t r q o", r=RUNS, t=TILES)[t])
        w3_raw = sb("w3_raw", [P, PACK, 512], F32)
        for u in range(2):
            nc.sync.dma_start(out=w3_raw[:, 2 * u : 2 * u + 2, :].rearrange("p e c -> p (e c)"), in_=w3.rearrange("(b u q e) c -> u b q (e c)", u=2, q=8, e=2)[u])

        ident = sb("ident", [P, P], F32)
        make_identity(nc, ident[:])

        a_win = [sb("a_win%d" % t, [P, 2 * S], F32) if VECTOR_DEN_LISTS[t] < 3 else None for t in range(TILES)]
        c_win = [sb("c_win%d" % t, [P, 2 * S], F32) if VECTOR_DEN_LISTS[t] > 0 else None for t in range(TILES)]
        p_win = [sb("p_win%d" % t, [P, 2 * S], F32) for t in range(TILES)]
        c_of = []
        for t in range(TILES):
            if c_win[t] is None:
                c_of.append(a_win[t][:, S:])
            else:
                c_of.append(c_win[t][:, :S])
                nc.gpsimd.memset(c_win[t][:, S:], 0.0)
                if a_win[t] is not None:
                    nc.gpsimd.memset(a_win[t][:, S:], 0.0)
            nc.gpsimd.memset(p_win[t][:, S:], 0.0)

        def pick(name, table, dtype, lst):
            picked = sb(name, [P, S], dtype)
            nc.vector.tensor_copy(picked[:], table[:].indirect(lst[:]))
            return picked

        def cast(engine, dst, src):
            if engine is nc.scalar:
                nc.scalar.copy(dst, src)
            else:
                engine.tensor_copy(dst, src)

        def cast_half(grouped, halves, h, engines):
            for t in range(TILES):
                if engines[t] is nc.gpsimd:
                    dst = grouped[t][:, 256 * h : 256 * (h + 1)].rearrange("p (r q j) -> p r q j", r=4, j=PACK)
                    src = halves[h][:].rearrange("p j (r t q) -> p t r q j", r=4, t=TILES)[:, t]
                    nc.gpsimd.tensor_scalar(dst, src, 1.0, 0.0, op0=ALU.mult, op1=ALU.add)
                else:
                    dst = grouped[t][:, 256 * h : 256 * (h + 1)].rearrange("p (r a i j) -> p r a j i", r=4, a=4, i=4)
                    src = halves[h][:].rearrange("p j (r t a i) -> p t r a j i", r=4, t=TILES, a=4)[:, t]
                    cast(engines[t], dst, src)

        def quantize_tile(name, grouped):
            codes = sb(name + "_c", [P, P], U32)
            scales = sb(name + "_s", [P, P], U8)
            nc.vector.quantize_mx(out=codes[:].bitcast(FP8X4), scales=scales[:], in_=grouped[:])
            return codes, scales

        def product(acc, lhs_codes, lhs_scales, rhs_codes, rhs_scales):
            nc.tensor.matmul_mx(out=acc, lhsT=lhs_codes.bitcast(FP8X4), lhsT_scale=lhs_scales,
                                rhs=rhs_codes.bitcast(FP8X4), rhs_scale=rhs_scales, start=True, stop=True)

        x2_words = pick("x2_words", x_tab, U32, two_l)
        x2_scales = pick("x2_scales", x_plane, U8, two_l)
        w2_g = [sb("w2_g%d" % t, [P, P * PACK], BF16) for t in range(TILES)]
        w1_all = sb("w1_all", [P, TILES * P * PACK], BF16)
        w1_g = [w1_all[:, t * 512 : (t + 1) * 512] for t in range(TILES)]
        cast_half(w2_g, w2_raw, 0, [nc.scalar] * TILES)
        cast_half(w2_g, w2_raw, 1, [nc.vector, nc.vector, nc.scalar, nc.scalar])
        w2_q = [quantize_tile("w2_%d" % t, w2_g[t]) for t in range(TILES)]
        cast_half(w1_g, w1_raw, 0, [nc.gpsimd] * TILES)
        x1_scales = pick("x1_scales", x_plane, U8, offs_l)
        x1_words = pick("x1_words", x_tab, U32, offs_l)
        a_bank = [bank(t, "a_bank%d" % t, [P, S]) for t in range(TILES)]
        for t in range(TILES):
            product(a_bank[t][:], w2_q[t][0][:], w2_q[t][1][:], x2_words[:], x2_scales[:])
            nc.scalar.activation(c_of[t], a_bank[t][:], ACT.Sigmoid)
            if a_win[t] is not None:
                nc.scalar.copy(a_win[t][:, :S], a_bank[t][:])

        cast_half(w1_g, w1_raw, 1, [nc.vector] * TILES)
        w1_codes = sb("w1_codes", [P, 512], U32)
        w1_scales = sb("w1_scales", [P, 512], U8)
        nc.vector.quantize_mx(out=w1_codes[:].bitcast(FP8X4), scales=w1_scales[:], in_=w1_all[:])
        y_bank = [bank(4 + t, "y_bank%d" % t, [P, S]) for t in range(TILES)]
        for t in range(TILES):
            product(y_bank[t][:], w1_codes[:, t * P : (t + 1) * P], w1_scales[:, t * P : (t + 1) * P], x1_words[:], x1_scales[:])

        def chunk(tile, jc):
            return tile[:, jc * P : (jc + 1) * P]

        den_log = sb("den_log", [P, CHUNKS, 2, RUNS, 2, GROUP], F32)
        num_bank = [None] * CHUNKS
        den_bank = [None] * TILES

        def den_tile(t):
            vols = []
            for n in range(3):
                vol = keep.tile([P, S], F32, name="vol%d_%d" % (t, n), tag="vol%d_%d" % (t, n), align_bytes=64)
                if n < VECTOR_DEN_LISTS[t]:
                    nc.vector.tensor_copy(vol[:], c_win[t][:].indirect(lists[n][:]))
                else:
                    nc.scalar.activation(vol[:], a_win[t][:].indirect(lists[n][:]), ACT.Sigmoid)
                vols.append(vol)
            den_bank[t] = bank(4 + t, "den_bank%d" % t, [P, CHUNKS, P])
            for jc in range(CHUNKS):
                for n in range(3):
                    nc.tensor.matmul(den_bank[t][:, jc, :], lhsT=chunk(vols[n], jc), rhs=ident[:], is_transpose=True, start=(n == 0), stop=(n == 2))

        def num_tile(t, identity):
            for n in range(3):
                paid = sb("paid%d_%d" % (t, n), [P, S], F32)
                nc.vector.tensor_copy(paid[:], p_win[t][:].indirect(lists[n][:]))
                for jc in range(CHUNKS):
                    nc.tensor.matmul(num_bank[jc][:, t % 2, :, t // 2, :], lhsT=chunk(paid, jc), rhs=identity[:], is_transpose=True, start=(n == 0), stop=(n == 2))

        for t in range(TILES):
            nc.vector.scalar_tensor_tensor(out=p_win[t][:, :S], in0=y_bank[t][:], scalar=gain[t][:], in1=c_of[t], op0=ALU.mult, op1=ALU.mult)
        for jc in range(CHUNKS):
            num_bank[jc] = bank(jc, "num_bank%d" % jc, [P, 2, RUNS, 2, GROUP])

        w3_g = sb("w3_g", [P, 512 * PACK], BF16)
        w3_codes = sb("w3_codes", [P, 512], U32)
        w3_scales = sb("w3_scales", [P, 512], U8)
        for t in range(TILES):
            den_tile(t)
        late_ident = keep.tile([P, P], F32, name="late_ident", tag="vol3_2", align_bytes=64)
        for t in range(TILES):
            nc.scalar.activation(den_log[:, :, t % 2, :, t // 2, :], den_bank[t][:].rearrange("p c (r q) -> p c r q", q=GROUP), ACT.Ln)
            if t == 0:
                nc.scalar.copy(late_ident[:], ident[:])
        for t in range(TILES):
            num_tile(t, ident if t < 2 else late_ident)
            if t == 0:
                nc.gpsimd.tensor_scalar(w3_g[:].rearrange("p (c j) -> p c j", j=PACK), w3_raw[:].rearrange("p j c -> p c j"), 1.0, 0.0, op0=ALU.mult, op1=ALU.add)
            if t == 2:
                nc.vector.quantize_mx(out=w3_codes[:].bitcast(FP8X4), scales=w3_scales[:], in_=w3_g[:])


        out_view = out.rearrange("(m p) j -> p m j", p=P)
        z_rows, z_group, z_codes, z_scales = [], [], [], []
        for jc in range(CHUNKS):
            inv = sb("inv%d" % jc, [P, S], F32)
            nc.scalar.activation(inv[:], den_log[:, jc].rearrange("p u r h q -> p (u r h q)"), ACT.Exp, scale=-1.0)
            z_rows.append(sb("z_rows%d" % jc, [P, S], BF16))
            nc.vector.tensor_tensor(out=z_rows[jc][:], in0=num_bank[jc][:].rearrange("p u r h q -> p (u r h q)"), in1=inv[:], op=ALU.mult)
        for jc in range(CHUNKS):
            back = bank(4 + jc % 2, "back%d" % jc, [P, 2, P])
            words = z_rows[jc][:].bitcast(F32)
            for u in range(2):
                nc.tensor.transpose(back[:, u, :], chunk(words, u), ident[:])
            z_group.append(sb("z_group%d" % jc, [P, P * PACK], BF16))
            nc.scalar.copy(z_group[jc][:].bitcast(F32).rearrange("p (j u) -> p j u", u=2), back[:].rearrange("p u j -> p j u"))
        for jc in range(CHUNKS):
            z_codes.append(sb("z_codes%d" % jc, [P, P], U32))
            z_scales.append(sb("z_scales%d" % jc, [P, P], U8))
            nc.vector.quantize_mx(out=z_codes[jc][:].bitcast(FP8X4), scales=z_scales[jc][:], in_=z_group[jc][:])
        for jc in range(CHUNKS):
            acc = bank(6 + jc % 2, "acc%d" % jc, [P, TILES, P])
            for m in range(TILES):
                product(acc[:, m, :], chunk(w3_codes, m), chunk(w3_scales, m), z_codes[jc][:], z_scales[jc][:])
            res = sb("res%d" % jc, [P, TILES, P], F32)
            cast(nc.scalar if jc < CHUNKS - 1 else nc.vector, res[:], acc[:])
            nc.sync.dma_start(out=out_view[:, :, jc * P : (jc + 1) * P], in_=res[:])
